import numpy as np
import ml_dtypes


def mxq(x, axis, fmt="e4m3"):
    dtype, down = {"e4m3": (ml_dtypes.float8_e4m3fn, 7), "e5m2": (ml_dtypes.float8_e5m2, 14)}[fmt]
    v = np.moveaxis(np.asarray(x, np.float32).astype(ml_dtypes.bfloat16).astype(np.float64), axis, -1)
    blocks = v.reshape(v.shape[:-1] + (-1, 32))
    amax = np.abs(blocks).max(-1, keepdims=True)
    byte = np.maximum(np.where(amax > 0, np.frexp(amax)[1] - 1 + 127, 0) - down, 1)
    scale = np.exp2(byte - 127.0)
    codes = (blocks / scale).astype(np.float32).astype(dtype).astype(np.float64)
    return np.moveaxis((codes * scale).reshape(v.shape), -1, axis)


WIDE = False


def mx_kscale(k):
    if not WIDE:
        return np.ones(k)
    levels = np.array([10, -10, 5, -5, 0])
    if k % 512:
        return np.exp2(np.random.permutation(np.resize(levels, k // 32))).repeat(32)
    a = np.empty((k // 512, 16))
    for p in range(k // 512):
        a[p, :8] = np.random.permutation(np.resize(levels, 8))
        for g in range(8):
            far = levels[np.abs(levels - a[p, g]) >= 10]
            a[p, g + 8] = far[np.random.randint(len(far))]
    return np.exp2(a.ravel()).repeat(32)


def f64(x):
    return np.asarray(x).astype(np.float64)


def striped(idx):
    return np.tile(np.asarray(idx).reshape(-1, 16).T, (8, 1)).astype(np.uint16)


def unstriped(offs):
    return offs[:16].T.reshape(-1).astype(np.int64)


E2M1 = np.array([0.0, 0.5, 1.0, 1.5, 2.0, 3.0, 4.0, 6.0, -0.0, -0.5, -1.0, -1.5, -2.0, -3.0, -4.0, -6.0])


def pack_weight(w, fmt):
    k, n = w.shape
    w = f64(np.asarray(w, np.float32).astype(ml_dtypes.bfloat16)).reshape(k // 32, 32, n)
    amax = np.abs(w).max(1)
    if fmt == "e4m3":
        byte = np.frexp(amax)[1] - 1 + 127 - 7
    else:
        mant, ex = np.frexp(amax / 6.0)
        byte = np.where(mant > 0.5, ex, ex - 1) + 127
    byte = np.clip(np.where(amax > 0, byte, 1), 1, 254)
    scaled = (w * np.exp2(127.0 - byte)[:, None, :]).reshape(k, n).astype(np.float32)
    by_word = np.ascontiguousarray(scaled.reshape(k // 512, 128, 4, n).transpose(0, 1, 3, 2))
    if fmt == "e4m3":
        words = by_word.astype(ml_dtypes.float8_e4m3fn).view(np.uint8)
    else:
        c = by_word.astype(ml_dtypes.float4_e2m1fn).view(np.uint8) & 0xF
        words = (c[..., 0::2] | (c[..., 1::2] << 4)).reshape(k // 512, 128, 2 * n)
    return np.ascontiguousarray(words), np.ascontiguousarray(byte.astype(np.uint8).reshape(k // 512, 16, n))


def unpack_weight(words, scales, fmt):
    g, _, n = scales.shape
    words = np.ascontiguousarray(words).reshape(g, 128, n, -1)
    if fmt == "e4m3":
        vals = words.view(ml_dtypes.float8_e4m3fn).astype(np.float64)
    else:
        nib = np.empty((g, 128, n, 4), np.uint8)
        nib[..., 0::2] = words & 0xF
        nib[..., 1::2] = words >> 4
        vals = E2M1[nib]
    vals = vals * np.repeat(np.exp2(scales.astype(np.float64) - 127.0), 8, axis=1)[..., None]
    return vals.transpose(0, 1, 3, 2).reshape(g * 512, n)


def softplus(v):
    return np.log(1.0 + np.exp(v))


D, K, R, T, I, Q = 512, 512, 512, 2048, 512, 128


def setup_inputs():
    n = np.random.standard_normal
    idx = np.random.permutation(T)[:I]
    fd = mx_kscale(D)
    fk = mx_kscale(K)
    fi = mx_kscale(I)
    keysp = pack_weight(n((D, T)) / fd[:, None], "e2m1")
    tabp = pack_weight(n((K, T)) / fk[:, None], "e2m1")
    return {
        "query": (n((D, Q)) * 0.9 / np.sqrt(D) * fd[:, None]).astype(np.float32),
        "keys_words": keysp[0],
        "keys_scales": keysp[1],
        "th": (np.random.uniform(-0.3, 0.6, (Q, 1))).astype(np.float32),
        "reserve": (np.random.uniform(50.0, 200.0, (Q, 1))).astype(np.float32),
        "tab_words": tabp[0],
        "tab_scales": tabp[1],
        "w1": (n((K, R)) * 1 / np.sqrt(K) * fk[:, None]).astype(np.float32),
        "gain": (np.random.uniform(0.5, 2.0, (R, 1))).astype(np.float32),
        "os": (np.random.uniform(4.0, 16.0, (1, I)) * fi).astype(np.float32),
        "vs": (np.random.uniform(0.5, 2.0, (1, I)) / fi).astype(np.float32),
        "offs": striped(idx),
    }


def reference(query, keys_words, keys_scales, th, reserve, tab_words, tab_scales, w1, gain, os, vs, offs):
    idx = unstriped(offs)
    keysu = unpack_weight(keys_words, keys_scales, "e2m1")
    tabu = unpack_weight(tab_words, tab_scales, "e2m1")
    queryq = mxq(f64(query), 0, "e4m3")
    keysidxg = keysu[:, idx]
    a = queryq.T @ keysidxg
    p = softplus(a - f64(th))
    z = np.sum(p, axis=1, keepdims=True) + f64(reserve)
    w = p / z
    w1q = mxq(f64(w1), 0, "e4m3")
    tabidxg = tabu[:, idx]
    zh = w1q.T @ tabidxg
    ht = np.tanh(zh)
    hv = ht * f64(gain)
    wo1 = w * f64(os)
    wt1 = wo1.T
    hw = hv * f64(vs)
    ht1 = hw.T
    wt1q = mxq(wt1, 0, "e4m3")
    ht1q = mxq(ht1, 0, "e4m3")
    o = wt1q.T @ ht1q
    return o

@@ -1,0 +1,182 @@
+from contextlib import ExitStack
+
+import concourse.mybir as mybir
+from concourse.masks import make_identity
+
+D, K, R, T, I, Q = 512, 512, 512, 2048, 512, 128
+FLOPS = 2 * (D * Q * I + K * R * I + I * Q * R)
+
+F32 = mybir.dt.float32
+BF16 = mybir.dt.bfloat16
+I32 = mybir.dt.int32
+U32 = mybir.dt.uint32
+U16 = mybir.dt.uint16
+U8 = mybir.dt.uint8
+FP8X4 = mybir.dt.float8_e4m3fn_x4
+FP4X4 = mybir.dt.float4_e2m1fn_x4
+ALU = mybir.AluOpType
+ACT = mybir.ActivationFunctionType
+
+P = 128
+PACK = 4
+CHUNKS = R // P
+HALF = R // 2
+TINY = 2.0 ** -60
+
+
+def tile_attend_lrgained_capped_kernel(tc, query, keys_words, keys_scales, th, reserve, tab_words, tab_scales,
+                                        w1, gain, slot_factor, value_scale, offs, out):
+    nc = tc.nc
+    with ExitStack() as ctx:
+        keep = ctx.enter_context(tc.tile_pool(name="keep", bufs=1))
+        ring = ctx.enter_context(tc.tile_pool(name="ring", bufs=2))
+        psum = ctx.enter_context(tc.psum_pool(name="psum", bufs=1))
+
+        def sb(name, shape, dtype):
+            return keep.tile(shape, dtype, name=name, align_bytes=64)
+
+        offsets = keep.tile([P, I // 16], U16, name="offsets")
+        nc.sync.dma_start(offsets[:], offs)
+
+        key_bytes = sb("key_bytes", [P, T], U8)
+        tab_bytes = sb("tab_bytes", [P, T], U8)
+        nc.vector.memset(key_bytes[:].bitcast(I32), 0)
+        nc.gpsimd.memset(tab_bytes[:].bitcast(I32), 0)
+
+        def load_bytes(queue, tile, scales):
+            rows = scales[0].rearrange("(a f) c -> f a c", f=4)
+            for f in range(4):
+                queue.dma_start(tile[f:P:32, :].bitcast(I32), rows[f].bitcast(I32))
+
+        load_bytes(nc.sync, key_bytes, keys_scales)
+        warm = sb("warm", [P, 1], F32)
+        warm_out = sb("warm_out", [P, 1], F32)
+        nc.vector.memset(warm[:], 0.0)
+        nc.scalar.activation(warm_out[:], warm[:], ACT.Sigmoid)
+
+        key_words = sb("key_words", [P, T], U16)
+        tab_wordst = sb("tab_wordst", [P, T], U16)
+        q_raw = sb("q_raw", [P, PACK, Q], F32)
+        nc.sync.dma_start(key_words[:].bitcast(I32), keys_words[0].bitcast(I32))
+        nc.sync.dma_start(q_raw[:], query.rearrange("(p j) q -> p j q", j=PACK))
+        nc.sync.dma_start(tab_wordst[:].bitcast(I32), tab_words[0].bitcast(I32))
+        w_raw = [sb("w_raw%d" % h, [P, PACK, HALF], F32) for h in range(2)]
+        w_rows = w1.rearrange("(p j) r -> p j r", j=PACK)
+        load_bytes(nc.sync, tab_bytes, tab_scales)
+        nc.sync.dma_start(w_raw[0][:], w_rows[:, :, 0:HALF])
+        nc.sync.dma_start(w_raw[1][:], w_rows[:, :, HALF:R])
+
+        th_col = sb("th_col", [P, 1], F32)
+        reserve_col = sb("reserve_col", [P, 1], F32)
+        os_cols = sb("os_cols", [P, PACK], F32)
+        vs_cols = sb("vs_cols", [P, PACK], F32)
+        gain_cols = sb("gain_cols", [P, CHUNKS], F32)
+        with nc.allow_non_contiguous_dma(reason="one value a partition"):
+            nc.gpsimd.dma_start(th_col[:], th)
+        identity = sb("identity", [P, P], F32)
+        make_identity(nc, identity[:])
+        nc.gpsimd.dma_start(os_cols[:], slot_factor.rearrange("o (p j) -> p (o j)", j=PACK))
+        nc.gpsimd.dma_start(vs_cols[:], value_scale.rearrange("o (p j) -> p (o j)", j=PACK))
+        with nc.allow_non_contiguous_dma(reason="one gain value a partition and chunk"):
+            nc.gpsimd.dma_start(reserve_col[:], reserve)
+            nc.sync.dma_start(gain_cols[:], gain.rearrange("(c p) o -> p (c o)", p=P))
+
+        key_g_bytes = sb("key_g_bytes", [P, I], U8)
+        key_g_words = sb("key_g_words", [P, I], U16)
+        nc.vector.tensor_copy(key_g_bytes[:], key_bytes[:].indirect(offsets[:]))
+        nc.vector.tensor_copy(key_g_words[:], key_words[:].indirect(offsets[:]))
+
+        q_grouped = sb("q_grouped", [P, Q, PACK], BF16)
+        nc.scalar.activation(q_grouped[:], q_raw[:].rearrange("p j q -> p q j"), ACT.Copy, scale=-1.0)
+        q_codes = sb("q_codes", [P, Q], U32)
+        q_bytes = sb("q_bytes", [P, Q], U8)
+        nc.vector.quantize_mx(q_codes[:].bitcast(FP8X4), q_bytes[:], q_grouped[:].rearrange("p q j -> p (q j)"))
+
+        neg_a = psum.tile([P, I], F32, name="neg_a", tag="bank_c")
+        nc.tensor.matmul_mx(neg_a[:], lhsT=q_codes[:].bitcast(FP8X4), lhsT_scale=q_bytes[:],
+                            rhs=key_g_words[:].bitcast(FP4X4), rhs_scale=key_g_bytes[:], start=True, stop=True)
+
+        os_spread = psum.tile([P, PACK, P], F32, name="os_spread", tag="bank_a")
+        vs_spread = psum.tile([P, PACK, P], F32, name="vs_spread", tag="bank_b")
+        for cols, spread in ((os_cols, os_spread), (vs_cols, vs_spread)):
+            for j in range(PACK):
+                nc.tensor.transpose(spread[:, j, :], cols[:, j:j + 1].to_broadcast([P, P]), identity[:])
+
+        sig = sb("sig", [P, I], F32)
+        nc.scalar.activation(sig[:], neg_a[:], ACT.Sigmoid, bias=th_col[:])
+        ln_sig = sb("ln_sig", [P, I], F32)
+        nc.scalar.activation(ln_sig[:], sig[:], ACT.Ln, bias=TINY)
+
+        tab_g_bytes = sb("tab_g_bytes", [P, I], U8)
+        tab_g_words = sb("tab_g_words", [P, I], U16)
+        nc.vector.tensor_copy(tab_g_words[:], tab_wordst[:].indirect(offsets[:]))
+        nc.vector.tensor_copy(tab_g_bytes[:], tab_bytes[:].indirect(offsets[:]))
+
+        w_codes = sb("w_codes", [P, R], U32)
+        w_bytes = sb("w_bytes", [P, R], U8)
+        w_grouped = [sb("w_grouped%d" % h, [P, HALF, PACK], BF16) for h in range(2)]
+        for h in range(2):
+            nc.vector.tensor_copy(w_grouped[h][:].rearrange("p (c i) t -> p c t i", i=4),
+                                  w_raw[h][:].rearrange("p t (c i) -> p c t i", i=4))
+        for h in range(2):
+            cols = slice(h * HALF, (h + 1) * HALF)
+            nc.vector.quantize_mx(w_codes[:, cols].bitcast(FP8X4), w_bytes[:, cols],
+                                  w_grouped[h][:].rearrange("p r j -> p (r j)"))
+
+        neg_p = sb("neg_p", [P, I], F32)
+        neg_sum = sb("neg_sum", [P, 1], F32)
+        nc.vector.scalar_tensor_tensor(neg_p[:], neg_a[:], th_col[:], ln_sig[:], ALU.add, ALU.min,
+                                       accum_out=neg_sum[:])
+        neg_z = sb("neg_z", [P, 1], F32)
+        nc.vector.tensor_sub(neg_z[:], neg_sum[:], reserve_col[:])
+        neg_rz = sb("neg_rz", [P, 1], F32)
+        nc.vector.reciprocal(neg_rz[:], neg_z[:])
+        wo = sb("wo", [P, I], BF16)
+        nc.vector.scalar_tensor_tensor(wo[:].rearrange("p (s j) -> p s j", j=PACK),
+                                       neg_p[:].rearrange("p (s j) -> p s j", j=PACK), neg_rz[:],
+                                       os_spread[:].rearrange("p j s -> p s j"), ALU.mult, ALU.mult)
+
+        def turn(rows, bank, grouped):
+            words = rows.bitcast(F32)
+            for u in range(2):
+                nc.tensor.transpose(bank[:, u, :], words[:, u::2], identity[:])
+            nc.scalar.copy(grouped[:].bitcast(F32), bank[:].rearrange("p u x -> p x u"))
+
+        ht = []
+        for c in range(CHUNKS):
+            cols = slice(c * P, (c + 1) * P)
+            zh = psum.tile([P, I], F32, name="zh", tag="zh", bufs=3)
+            nc.tensor.matmul_mx(zh[:], lhsT=w_codes[:, cols].bitcast(FP8X4), lhsT_scale=w_bytes[:, cols],
+                                rhs=tab_g_words[:].bitcast(FP4X4), rhs_scale=tab_g_bytes[:], start=True, stop=True)
+            ht.append(sb("ht%d" % c, [P, I], F32))
+            nc.scalar.activation(ht[c][:], zh[:], ACT.Tanh)
+        wt_bank = psum.tile([P, 2, P], F32, name="wt_bank", tag="zh", bufs=3)
+        wt_grouped = sb("wt_grouped", [P, Q, PACK], BF16)
+        turn(wo[:], wt_bank, wt_grouped)
+        wt_codes = sb("wt_codes", [P, Q], U32)
+        wt_bytes = sb("wt_bytes", [P, Q], U8)
+        nc.vector.quantize_mx(wt_codes[:].bitcast(FP8X4), wt_bytes[:], wt_grouped[:].rearrange("p q j -> p (q j)"))
+
+        ht_grouped = []
+        for c in range(CHUNKS):
+            hw = sb("hw%d" % c, [P, I], BF16)
+            nc.vector.scalar_tensor_tensor(hw[:].rearrange("p (s j) -> p s j", j=PACK),
+                                           ht[c][:].rearrange("p (s j) -> p s j", j=PACK), gain_cols[:, c:c + 1],
+                                           vs_spread[:].rearrange("p j s -> p s j"), ALU.mult, ALU.mult)
+            ht_bank = psum.tile([P, 2, P], F32, name="ht_bank", tag="ht_bank", bufs=2)
+            ht_grouped.append(sb("ht_grouped%d" % c, [P, P, PACK], BF16))
+            turn(hw[:], ht_bank, ht_grouped[c])
+        result = sb("result", [P, R], F32)
+        for c in range(CHUNKS):
+            cols = slice(c * P, (c + 1) * P)
+            ht_codes = sb("ht_codes%d" % c, [P, P], U32)
+            ht_bytes = sb("ht_bytes%d" % c, [P, P], U8)
+            nc.vector.quantize_mx(ht_codes[:].bitcast(FP8X4), ht_bytes[:],
+                                  ht_grouped[c][:].rearrange("p r j -> p (r j)"))
+            o_bank = psum.tile([P, P], F32, name="o_bank", tag="bank_a" if c % 2 == 0 else "bank_c")
+            nc.tensor.matmul_mx(o_bank[:], lhsT=wt_codes[:].bitcast(FP8X4), lhsT_scale=wt_bytes[:],
+                                rhs=ht_codes[:].bitcast(FP8X4), rhs_scale=ht_bytes[:], start=True, stop=True)
+            nc.scalar.copy(result[:, cols], o_bank[:])
+            if c == CHUNKS - 2:
+                nc.sync.dma_start(out[:, 0:(c + 1) * P], result[:, 0:(c + 1) * P])
+        nc.sync.dma_start(out[:, R - P:R], result[:, R - P:R])

@@ -60,7 +60,8 @@ def tile_attend_lrgained_capped_kernel(tc, query, keys_words, keys_scales, th, r
         nc.sync.dma_start(key_words[:].bitcast(I32), keys_words[0].bitcast(I32))
         nc.sync.dma_start(q_raw[:], query.rearrange("(p j) q -> p j q", j=PACK))
         nc.sync.dma_start(tab_wordst[:].bitcast(I32), tab_words[0].bitcast(I32))
-        w_raw = [sb("w_raw%d" % h, [P, PACK, HALF], F32) for h in range(2)]
+        w_raw = [keep.tile([P, PACK, HALF], F32, name="w_raw%d" % h, tag="w_raw%d" % h, align_bytes=64)
+                 for h in range(2)]
         w_rows = w1.rearrange("(p j) r -> p j r", j=PACK)
         load_bytes(nc.sync, tab_bytes, tab_scales)
         nc.sync.dma_start(w_raw[0][:], w_rows[:, :, 0:HALF])
@@ -98,9 +99,11 @@ def tile_attend_lrgained_capped_kernel(tc, query, keys_words, keys_scales, th, r
 
         os_spread = psum.tile([P, PACK, P], F32, name="os_spread", tag="bank_a")
         vs_spread = psum.tile([P, PACK, P], F32, name="vs_spread", tag="bank_b")
-        for cols, spread in ((os_cols, os_spread), (vs_cols, vs_spread)):
-            for j in range(PACK):
-                nc.tensor.transpose(spread[:, j, :], cols[:, j:j + 1].to_broadcast([P, P]), identity[:])
+        for j in range(PACK):
+            nc.tensor.transpose(os_spread[:, j, :], os_cols[:, j:j + 1].to_broadcast([P, P]), identity[:])
+        for j in range(PACK):
+            nc.tensor.transpose(vs_spread[:, 2 * (j % 2) + j // 2, :], vs_cols[:, j:j + 1].to_broadcast([P, P]),
+                                identity[:])
 
         sig = sb("sig", [P, I], F32)
         nc.scalar.activation(sig[:], neg_a[:], ACT.Sigmoid, bias=th_col[:])
@@ -123,7 +126,7 @@ def tile_attend_lrgained_capped_kernel(tc, query, keys_words, keys_scales, th, r
             nc.vector.quantize_mx(w_codes[:, cols].bitcast(FP8X4), w_bytes[:, cols],
                                   w_grouped[h][:].rearrange("p r j -> p (r j)"))
 
-        neg_p = sb("neg_p", [P, I], F32)
+        neg_p = keep.tile([P, I], F32, name="neg_p", tag="w_raw1", align_bytes=64)
         neg_sum = sb("neg_sum", [P, 1], F32)
         nc.vector.scalar_tensor_tensor(neg_p[:], neg_a[:], th_col[:], ln_sig[:], ALU.add, ALU.min,
                                        accum_out=neg_sum[:])
@@ -136,10 +139,9 @@ def tile_attend_lrgained_capped_kernel(tc, query, keys_words, keys_scales, th, r
                                        neg_p[:].rearrange("p (s j) -> p s j", j=PACK), neg_rz[:],
                                        os_spread[:].rearrange("p j s -> p s j"), ALU.mult, ALU.mult)
 
-        def turn(rows, bank, grouped):
-            words = rows.bitcast(F32)
+        def turn(halves, bank, grouped):
             for u in range(2):
-                nc.tensor.transpose(bank[:, u, :], words[:, u::2], identity[:])
+                nc.tensor.transpose(bank[:, u, :], halves[u], identity[:])
             nc.scalar.copy(grouped[:].bitcast(F32), bank[:].rearrange("p u x -> p x u"))
 
         ht = []
@@ -149,10 +151,11 @@ def tile_attend_lrgained_capped_kernel(tc, query, keys_words, keys_scales, th, r
             nc.tensor.matmul_mx(zh[:], lhsT=w_codes[:, cols].bitcast(FP8X4), lhsT_scale=w_bytes[:, cols],
                                 rhs=tab_g_words[:].bitcast(FP4X4), rhs_scale=tab_g_bytes[:], start=True, stop=True)
             ht.append(sb("ht%d" % c, [P, I], F32))
-            nc.scalar.activation(ht[c][:], zh[:], ACT.Tanh)
+            nc.scalar.activation(ht[c][:].rearrange("p (u s e) -> p u s e", u=2, e=2),
+                                 zh[:].rearrange("p (s u e) -> p u s e", u=2, e=2), ACT.Tanh)
         wt_bank = psum.tile([P, 2, P], F32, name="wt_bank", tag="zh", bufs=3)
         wt_grouped = sb("wt_grouped", [P, Q, PACK], BF16)
-        turn(wo[:], wt_bank, wt_grouped)
+        turn([wo[:].bitcast(F32)[:, u::2] for u in range(2)], wt_bank, wt_grouped)
         wt_codes = sb("wt_codes", [P, Q], U32)
         wt_bytes = sb("wt_bytes", [P, Q], U8)
         nc.vector.quantize_mx(wt_codes[:].bitcast(FP8X4), wt_bytes[:], wt_grouped[:].rearrange("p q j -> p (q j)"))
@@ -160,12 +163,12 @@ def tile_attend_lrgained_capped_kernel(tc, query, keys_words, keys_scales, th, r
         ht_grouped = []
         for c in range(CHUNKS):
             hw = sb("hw%d" % c, [P, I], BF16)
-            nc.vector.scalar_tensor_tensor(hw[:].rearrange("p (s j) -> p s j", j=PACK),
-                                           ht[c][:].rearrange("p (s j) -> p s j", j=PACK), gain_cols[:, c:c + 1],
-                                           vs_spread[:].rearrange("p j s -> p s j"), ALU.mult, ALU.mult)
+            nc.vector.scalar_tensor_tensor(hw[:].rearrange("p (x e) -> p x e", e=2),
+                                           ht[c][:].rearrange("p (x e) -> p x e", e=2), gain_cols[:, c:c + 1],
+                                           vs_spread[:].rearrange("p (e u) s -> p (u s) e", e=2), ALU.mult, ALU.mult)
             ht_bank = psum.tile([P, 2, P], F32, name="ht_bank", tag="ht_bank", bufs=2)
             ht_grouped.append(sb("ht_grouped%d" % c, [P, P, PACK], BF16))
-            turn(hw[:], ht_bank, ht_grouped[c])
+            turn([hw[:].bitcast(F32)[:, u * P:(u + 1) * P] for u in range(2)], ht_bank, ht_grouped[c])
         result = sb("result", [P, R], F32)
         for c in range(CHUNKS):
             cols = slice(c * P, (c + 1) * P)
@@ -179,4 +182,4 @@ def tile_attend_lrgained_capped_kernel(tc, query, keys_words, keys_scales, th, r
             nc.scalar.copy(result[:, cols], o_bank[:])
             if c == CHUNKS - 2:
                 nc.sync.dma_start(out[:, 0:(c + 1) * P], result[:, 0:(c + 1) * P])
-        nc.sync.dma_start(out[:, R - P:R], result[:, R - P:R])
+        nc.scalar.dma_start(out[:, R - P:R], result[:, R - P:R])

@@ -19,9 +19,18 @@ ACT = mybir.ActivationFunctionType
 
 P = 128
 PACK = 4
+QUADRANT = 32
+SCALE_ROWS = 4
+LIST_ROWS = 16
 CHUNKS = R // P
-HALF = R // 2
+LAST = CHUNKS - 1
 TINY = 2.0 ** -60
+ZH_BANKS = 3
+TURN_BANKS = 2
+
+
+def halves(n):
+    return [slice(0, n // 2), slice(n // 2, n)]
 
 
 def tile_attend_lrgained_capped_kernel(tc, query, keys_words, keys_scales, th, reserve, tab_words, tab_scales,
@@ -29,157 +38,160 @@ def tile_attend_lrgained_capped_kernel(tc, query, keys_words, keys_scales, th, r
     nc = tc.nc
     with ExitStack() as ctx:
         keep = ctx.enter_context(tc.tile_pool(name="keep", bufs=1))
-        ring = ctx.enter_context(tc.tile_pool(name="ring", bufs=2))
         psum = ctx.enter_context(tc.psum_pool(name="psum", bufs=1))
 
-        def sb(name, shape, dtype):
-            return keep.tile(shape, dtype, name=name, align_bytes=64)
+        def sbuf(name, shape, dtype, tag=None):
+            return keep.tile(shape, dtype, name=name, tag=tag or name, align_bytes=64)
 
-        offsets = keep.tile([P, I // 16], U16, name="offsets")
+        def bank(name, shape, tag):
+            return psum.tile(shape, F32, name=name, tag=tag, bufs={"zh": ZH_BANKS, "turned": TURN_BANKS}.get(tag, 1))
+
+        def quantise(codes, scale_bytes, grouped):
+            nc.vector.quantize_mx(codes.bitcast(FP8X4), scale_bytes, grouped.rearrange("p c t -> p (c t)"))
+
+        offsets = keep.tile([P, I // LIST_ROWS], U16, name="offsets")
         nc.sync.dma_start(offsets[:], offs)
 
-        key_bytes = sb("key_bytes", [P, T], U8)
-        tab_bytes = sb("tab_bytes", [P, T], U8)
-        nc.vector.memset(key_bytes[:].bitcast(I32), 0)
-        nc.gpsimd.memset(tab_bytes[:].bitcast(I32), 0)
+        key_pool_bytes = sbuf("key_pool_bytes", [P, T], U8)
+        tab_pool_bytes = sbuf("tab_pool_bytes", [P, T], U8)
+        nc.vector.memset(key_pool_bytes[:].bitcast(I32), 0)
+        nc.vector.memset(tab_pool_bytes[:].bitcast(I32), 0)
 
-        def load_bytes(queue, tile, scales):
-            rows = scales[0].rearrange("(a f) c -> f a c", f=4)
-            for f in range(4):
-                queue.dma_start(tile[f:P:32, :].bitcast(I32), rows[f].bitcast(I32))
+        def load_scale_rows(pool_bytes, scales):
+            rows = scales[0].rearrange("(a f) c -> f a c", f=SCALE_ROWS)
+            for f in range(SCALE_ROWS):
+                nc.sync.dma_start(pool_bytes[f:P:QUADRANT, :].bitcast(I32), rows[f].bitcast(I32))
 
-        load_bytes(nc.sync, key_bytes, keys_scales)
-        warm = sb("warm", [P, 1], F32)
-        warm_out = sb("warm_out", [P, 1], F32)
-        nc.vector.memset(warm[:], 0.0)
-        nc.scalar.activation(warm_out[:], warm[:], ACT.Sigmoid)
+        load_scale_rows(key_pool_bytes, keys_scales)
+        key_pool_words = sbuf("key_pool_words", [P, T], U16)
+        tab_pool_words = sbuf("tab_pool_words", [P, T], U16)
+        query_rows = sbuf("query_rows", [P, PACK, Q], F32)
+        nc.sync.dma_start(query_rows[:], query.rearrange("(p t) q -> p t q", t=PACK))
+        nc.sync.dma_start(key_pool_words[:].bitcast(I32), keys_words[0].bitcast(I32))
+        nc.sync.dma_start(tab_pool_words[:].bitcast(I32), tab_words[0].bitcast(I32))
+        w1_rows = sbuf("w1_rows", [P, PACK, R], F32)
+        load_scale_rows(tab_pool_bytes, tab_scales)
+        nc.sync.dma_start(w1_rows[:], w1.rearrange("(p t) r -> p t r", t=PACK))
 
-        key_words = sb("key_words", [P, T], U16)
-        tab_wordst = sb("tab_wordst", [P, T], U16)
-        q_raw = sb("q_raw", [P, PACK, Q], F32)
-        nc.sync.dma_start(key_words[:].bitcast(I32), keys_words[0].bitcast(I32))
-        nc.sync.dma_start(q_raw[:], query.rearrange("(p j) q -> p j q", j=PACK))
-        nc.sync.dma_start(tab_wordst[:].bitcast(I32), tab_words[0].bitcast(I32))
-        w_raw = [keep.tile([P, PACK, HALF], F32, name="w_raw%d" % h, tag="w_raw%d" % h, align_bytes=64)
-                 for h in range(2)]
-        w_rows = w1.rearrange("(p j) r -> p j r", j=PACK)
-        load_bytes(nc.sync, tab_bytes, tab_scales)
-        nc.sync.dma_start(w_raw[0][:], w_rows[:, :, 0:HALF])
-        nc.sync.dma_start(w_raw[1][:], w_rows[:, :, HALF:R])
-
-        th_col = sb("th_col", [P, 1], F32)
-        reserve_col = sb("reserve_col", [P, 1], F32)
-        os_cols = sb("os_cols", [P, PACK], F32)
-        vs_cols = sb("vs_cols", [P, PACK], F32)
-        gain_cols = sb("gain_cols", [P, CHUNKS], F32)
+        th_col = sbuf("th_col", [P, 1], F32)
+        reserve_col = sbuf("reserve_col", [P, 1], F32)
+        os_cols = sbuf("os_cols", [P, PACK], F32)
+        vs_cols = sbuf("vs_cols", [P, PACK], F32)
+        gain_cols = sbuf("gain_cols", [P, CHUNKS], F32)
         with nc.allow_non_contiguous_dma(reason="one value a partition"):
             nc.gpsimd.dma_start(th_col[:], th)
-        identity = sb("identity", [P, P], F32)
+        identity = sbuf("identity", [P, P], F32)
         make_identity(nc, identity[:])
-        nc.gpsimd.dma_start(os_cols[:], slot_factor.rearrange("o (p j) -> p (o j)", j=PACK))
-        nc.gpsimd.dma_start(vs_cols[:], value_scale.rearrange("o (p j) -> p (o j)", j=PACK))
-        with nc.allow_non_contiguous_dma(reason="one gain value a partition and chunk"):
+        nc.gpsimd.dma_start(os_cols[:], slot_factor.rearrange("o (s t) -> s (o t)", t=PACK))
+        nc.gpsimd.dma_start(vs_cols[:], value_scale.rearrange("o (s t) -> s (o t)", t=PACK))
+        with nc.allow_non_contiguous_dma(reason="one value a partition (and chunk)"):
             nc.gpsimd.dma_start(reserve_col[:], reserve)
             nc.sync.dma_start(gain_cols[:], gain.rearrange("(c p) o -> p (c o)", p=P))
 
-        key_g_bytes = sb("key_g_bytes", [P, I], U8)
-        key_g_words = sb("key_g_words", [P, I], U16)
-        nc.vector.tensor_copy(key_g_bytes[:], key_bytes[:].indirect(offsets[:]))
-        nc.vector.tensor_copy(key_g_words[:], key_words[:].indirect(offsets[:]))
+        key_bytes = sbuf("key_bytes", [P, I], U8)
+        key_words = sbuf("key_words", [P, I], U16)
+        nc.vector.tensor_copy(key_bytes[:], key_pool_bytes[:].indirect(offsets[:]))
 
-        q_grouped = sb("q_grouped", [P, Q, PACK], BF16)
-        nc.scalar.activation(q_grouped[:], q_raw[:].rearrange("p j q -> p q j"), ACT.Copy, scale=-1.0)
-        q_codes = sb("q_codes", [P, Q], U32)
-        q_bytes = sb("q_bytes", [P, Q], U8)
-        nc.vector.quantize_mx(q_codes[:].bitcast(FP8X4), q_bytes[:], q_grouped[:].rearrange("p q j -> p (q j)"))
+        neg_query = sbuf("neg_query", [P, Q, PACK], BF16)
+        nc.vector.tensor_scalar(neg_query[:], query_rows[:].rearrange("p t q -> p q t"), -1.0, None, ALU.mult)
+        query_codes = sbuf("query_codes", [P, Q], U32)
+        query_bytes = sbuf("query_bytes", [P, Q], U8)
+        quantise(query_codes[:], query_bytes[:], neg_query[:])
 
-        neg_a = psum.tile([P, I], F32, name="neg_a", tag="bank_c")
-        nc.tensor.matmul_mx(neg_a[:], lhsT=q_codes[:].bitcast(FP8X4), lhsT_scale=q_bytes[:],
-                            rhs=key_g_words[:].bitcast(FP4X4), rhs_scale=key_g_bytes[:], start=True, stop=True)
+        neg_a = [bank("neg_a0", [P, I // 2], "scores"), bank("neg_a1", [P, I // 2], "turned")]
+        sigmoid = sbuf("sigmoid", [P, I], F32)
+        for half_a, slots, columns in zip(neg_a, halves(I), halves(I // LIST_ROWS)):
+            nc.vector.tensor_copy(key_words[:, slots], key_pool_words[:].indirect(offsets[:, columns]))
+            nc.tensor.matmul_mx(half_a[:], lhsT=query_codes[:].bitcast(FP8X4), lhsT_scale=query_bytes[:],
+                                rhs=key_words[:, slots].bitcast(FP4X4), rhs_scale=key_bytes[:, slots],
+                                start=True, stop=True)
+            nc.scalar.activation(sigmoid[:, slots], half_a[:], ACT.Sigmoid, bias=th_col[:])
 
-        os_spread = psum.tile([P, PACK, P], F32, name="os_spread", tag="bank_a")
-        vs_spread = psum.tile([P, PACK, P], F32, name="vs_spread", tag="bank_b")
-        for j in range(PACK):
-            nc.tensor.transpose(os_spread[:, j, :], os_cols[:, j:j + 1].to_broadcast([P, P]), identity[:])
-        for j in range(PACK):
-            nc.tensor.transpose(vs_spread[:, 2 * (j % 2) + j // 2, :], vs_cols[:, j:j + 1].to_broadcast([P, P]),
-                                identity[:])
+        os_spread = bank("os_spread", [P, PACK, P], "os")
+        vs_spread = bank("vs_spread", [P, PACK, P], "vs")
+        for t in range(PACK):
+            nc.tensor.transpose(os_spread[:, t, :], os_cols[:, t:t + 1].to_broadcast([P, P]), identity[:])
+        for t in range(PACK):
+            u, e = divmod(t, 2)
+            nc.tensor.transpose(vs_spread[:, 2 * e + u, :], vs_cols[:, t:t + 1].to_broadcast([P, P]), identity[:])
 
-        sig = sb("sig", [P, I], F32)
-        nc.scalar.activation(sig[:], neg_a[:], ACT.Sigmoid, bias=th_col[:])
-        ln_sig = sb("ln_sig", [P, I], F32)
-        nc.scalar.activation(ln_sig[:], sig[:], ACT.Ln, bias=TINY)
+        ln_sigmoid = sbuf("ln_sigmoid", [P, I], F32)
+        nc.scalar.activation(ln_sigmoid[:], sigmoid[:], ACT.Ln, bias=TINY)
 
-        tab_g_bytes = sb("tab_g_bytes", [P, I], U8)
-        tab_g_words = sb("tab_g_words", [P, I], U16)
-        nc.vector.tensor_copy(tab_g_words[:], tab_wordst[:].indirect(offsets[:]))
-        nc.vector.tensor_copy(tab_g_bytes[:], tab_bytes[:].indirect(offsets[:]))
+        tab_bytes = sbuf("tab_bytes", [P, I], U8)
+        tab_listed_words = sbuf("tab_listed_words", [P, I], U16)
+        nc.vector.tensor_copy(tab_listed_words[:], tab_pool_words[:].indirect(offsets[:]))
+        nc.vector.tensor_copy(tab_bytes[:], tab_pool_bytes[:].indirect(offsets[:]))
 
-        w_codes = sb("w_codes", [P, R], U32)
-        w_bytes = sb("w_bytes", [P, R], U8)
-        w_grouped = [sb("w_grouped%d" % h, [P, HALF, PACK], BF16) for h in range(2)]
-        for h in range(2):
-            nc.vector.tensor_copy(w_grouped[h][:].rearrange("p (c i) t -> p c t i", i=4),
-                                  w_raw[h][:].rearrange("p t (c i) -> p c t i", i=4))
-        for h in range(2):
-            cols = slice(h * HALF, (h + 1) * HALF)
-            nc.vector.quantize_mx(w_codes[:, cols].bitcast(FP8X4), w_bytes[:, cols],
-                                  w_grouped[h][:].rearrange("p r j -> p (r j)"))
+        w1_codes = sbuf("w1_codes", [P, R], U32)
+        w1_bytes = sbuf("w1_bytes", [P, R], U8)
+        w1_grouped = [sbuf("w1_grouped%d" % h, [P, R // 2, PACK], BF16) for h in range(2)]
+        for grouped, cols in zip(w1_grouped, halves(R)):
+            nc.vector.tensor_copy(grouped[:].rearrange("p (c n) t -> p c t n", n=4),
+                                  w1_rows[:, :, cols].rearrange("p t (c n) -> p c t n", n=4))
+        first, second = halves(R)
+        quantise(w1_codes[:, first], w1_bytes[:, first], w1_grouped[0][:])
 
-        neg_p = keep.tile([P, I], F32, name="neg_p", tag="w_raw1", align_bytes=64)
-        neg_sum = sb("neg_sum", [P, 1], F32)
-        nc.vector.scalar_tensor_tensor(neg_p[:], neg_a[:], th_col[:], ln_sig[:], ALU.add, ALU.min,
-                                       accum_out=neg_sum[:])
-        neg_z = sb("neg_z", [P, 1], F32)
-        nc.vector.tensor_sub(neg_z[:], neg_sum[:], reserve_col[:])
-        neg_rz = sb("neg_rz", [P, 1], F32)
-        nc.vector.reciprocal(neg_rz[:], neg_z[:])
-        wo = sb("wo", [P, I], BF16)
-        nc.vector.scalar_tensor_tensor(wo[:].rearrange("p (s j) -> p s j", j=PACK),
-                                       neg_p[:].rearrange("p (s j) -> p s j", j=PACK), neg_rz[:],
-                                       os_spread[:].rearrange("p j s -> p s j"), ALU.mult, ALU.mult)
+        neg_p = sbuf("neg_p", [P, I], F32, tag="w1_rows")
+        neg_sums = [sbuf("neg_sum%d" % h, [P, 1], F32) for h in range(2)]
+        for half_a, slots, neg_sum in zip(neg_a, halves(I), neg_sums):
+            nc.vector.scalar_tensor_tensor(neg_p[:, slots], half_a[:], th_col[:], ln_sigmoid[:, slots],
+                                           ALU.add, ALU.min, accum_out=neg_sum[:])
+        quantise(w1_codes[:, second], w1_bytes[:, second], w1_grouped[1][:])
+        neg_z = sbuf("neg_z", [P, 1], F32)
+        nc.vector.tensor_scalar(neg_z[:], neg_sums[0][:], neg_sums[1][:], reserve_col[:], ALU.add, ALU.subtract)
+        neg_inv_z = sbuf("neg_inv_z", [P, 1], F32)
+        nc.vector.reciprocal(neg_inv_z[:], neg_z[:])
+        wo1 = sbuf("wo1", [P, I], BF16)
+        nc.vector.scalar_tensor_tensor(wo1[:].rearrange("p (s t) -> p s t", t=PACK),
+                                       neg_p[:].rearrange("p (s t) -> p s t", t=PACK), neg_inv_z[:],
+                                       os_spread[:].rearrange("p t s -> p s t"), ALU.mult, ALU.mult)
 
-        def turn(halves, bank, grouped):
+        def turn(pairs, turned, grouped):
             for u in range(2):
-                nc.tensor.transpose(bank[:, u, :], halves[u], identity[:])
-            nc.scalar.copy(grouped[:].bitcast(F32), bank[:].rearrange("p u x -> p x u"))
+                nc.tensor.transpose(turned[:, u, :], pairs[u], identity[:])
+            nc.scalar.copy(grouped[:].bitcast(F32), turned[:].rearrange("s u x -> s x u"))
 
         ht = []
         for c in range(CHUNKS):
             cols = slice(c * P, (c + 1) * P)
-            zh = psum.tile([P, I], F32, name="zh", tag="zh", bufs=3)
-            nc.tensor.matmul_mx(zh[:], lhsT=w_codes[:, cols].bitcast(FP8X4), lhsT_scale=w_bytes[:, cols],
-                                rhs=tab_g_words[:].bitcast(FP4X4), rhs_scale=tab_g_bytes[:], start=True, stop=True)
-            ht.append(sb("ht%d" % c, [P, I], F32))
+            zh = bank("zh", [P, I], "zh")
+            nc.tensor.matmul_mx(zh[:], lhsT=w1_codes[:, cols].bitcast(FP8X4), lhsT_scale=w1_bytes[:, cols],
+                                rhs=tab_listed_words[:].bitcast(FP4X4), rhs_scale=tab_bytes[:], start=True, stop=True)
+            ht.append(sbuf("ht%d" % c, [P, I], F32))
             nc.scalar.activation(ht[c][:].rearrange("p (u s e) -> p u s e", u=2, e=2),
                                  zh[:].rearrange("p (s u e) -> p u s e", u=2, e=2), ACT.Tanh)
-        wt_bank = psum.tile([P, 2, P], F32, name="wt_bank", tag="zh", bufs=3)
-        wt_grouped = sb("wt_grouped", [P, Q, PACK], BF16)
-        turn([wo[:].bitcast(F32)[:, u::2] for u in range(2)], wt_bank, wt_grouped)
-        wt_codes = sb("wt_codes", [P, Q], U32)
-        wt_bytes = sb("wt_bytes", [P, Q], U8)
-        nc.vector.quantize_mx(wt_codes[:].bitcast(FP8X4), wt_bytes[:], wt_grouped[:].rearrange("p q j -> p (q j)"))
 
-        ht_grouped = []
+        wt1_turned = bank("wt1_turned", [P, 2, Q], "zh")
+        wt1_grouped = sbuf("wt1_grouped", [P, Q, PACK], BF16)
+        turn([wo1[:].bitcast(F32)[:, u::2] for u in range(2)], wt1_turned, wt1_grouped)
+        wt1_codes = sbuf("wt1_codes", [P, Q], U32)
+        wt1_bytes = sbuf("wt1_bytes", [P, Q], U8)
+        quantise(wt1_codes[:], wt1_bytes[:], wt1_grouped[:])
+
+        ht1_grouped = []
         for c in range(CHUNKS):
-            hw = sb("hw%d" % c, [P, I], BF16)
-            nc.vector.scalar_tensor_tensor(hw[:].rearrange("p (x e) -> p x e", e=2),
-                                           ht[c][:].rearrange("p (x e) -> p x e", e=2), gain_cols[:, c:c + 1],
-                                           vs_spread[:].rearrange("p (e u) s -> p (u s) e", e=2), ALU.mult, ALU.mult)
-            ht_bank = psum.tile([P, 2, P], F32, name="ht_bank", tag="ht_bank", bufs=2)
-            ht_grouped.append(sb("ht_grouped%d" % c, [P, P, PACK], BF16))
-            turn([hw[:].bitcast(F32)[:, u * P:(u + 1) * P] for u in range(2)], ht_bank, ht_grouped[c])
-        result = sb("result", [P, R], F32)
+            hw = sbuf("hw%d" % c, [P, I], BF16)
+            for part in (halves(2 * P) if c == LAST else [slice(0, 2 * P)]):
+                nc.vector.scalar_tensor_tensor(hw[:].rearrange("p (x e) -> p x e", e=2)[:, part, :],
+                                               ht[c][:].rearrange("p (x e) -> p x e", e=2)[:, part, :],
+                                               gain_cols[:, c:c + 1],
+                                               vs_spread[:].rearrange("p (e u) s -> p (u s) e", e=2)[:, part, :],
+                                               ALU.mult, ALU.mult)
+            ht1_turned = bank("ht1_turned", [P, 2, P], "turned")
+            ht1_grouped.append(sbuf("ht1_grouped%d" % c, [P, P, PACK], BF16))
+            turn([hw[:].bitcast(F32)[:, part] for part in halves(2 * P)], ht1_turned, ht1_grouped[c])
+
+        result = sbuf("result", [P, R], F32)
         for c in range(CHUNKS):
             cols = slice(c * P, (c + 1) * P)
-            ht_codes = sb("ht_codes%d" % c, [P, P], U32)
-            ht_bytes = sb("ht_bytes%d" % c, [P, P], U8)
-            nc.vector.quantize_mx(ht_codes[:].bitcast(FP8X4), ht_bytes[:],
-                                  ht_grouped[c][:].rearrange("p r j -> p (r j)"))
-            o_bank = psum.tile([P, P], F32, name="o_bank", tag="bank_a" if c % 2 == 0 else "bank_c")
-            nc.tensor.matmul_mx(o_bank[:], lhsT=wt_codes[:].bitcast(FP8X4), lhsT_scale=wt_bytes[:],
-                                rhs=ht_codes[:].bitcast(FP8X4), rhs_scale=ht_bytes[:], start=True, stop=True)
-            nc.scalar.copy(result[:, cols], o_bank[:])
-            if c == CHUNKS - 2:
-                nc.sync.dma_start(out[:, 0:(c + 1) * P], result[:, 0:(c + 1) * P])
-        nc.scalar.dma_start(out[:, R - P:R], result[:, R - P:R])
+            ht1_codes = sbuf("ht1_codes%d" % c, [P, P], U32)
+            ht1_bytes = sbuf("ht1_bytes%d" % c, [P, P], U8)
+            quantise(ht1_codes[:], ht1_bytes[:], ht1_grouped[c][:])
+            sums = bank("sums", [P, P], ("os", "scores")[c % 2])
+            nc.tensor.matmul_mx(sums[:], lhsT=wt1_codes[:].bitcast(FP8X4), lhsT_scale=wt1_bytes[:],
+                                rhs=ht1_codes[:].bitcast(FP8X4), rhs_scale=ht1_bytes[:], start=True, stop=True)
+            nc.scalar.copy(result[:, cols], sums[:])
+            if c == LAST - 1:
+                nc.sync.dma_start(out[:, 0:LAST * P], result[:, 0:LAST * P])
+        nc.scalar.dma_start(out[:, LAST * P:R], result[:, LAST * P:R])

@@ -57,6 +57,11 @@ def tile_attend_lrgained_capped_kernel(tc, query, keys_words, keys_scales, th, r
         nc.vector.memset(key_pool_bytes[:].bitcast(I32), 0)
         nc.vector.memset(tab_pool_bytes[:].bitcast(I32), 0)
 
+        warm_in = sbuf("warm_in", [P, 1], F32)
+        warm_out = sbuf("warm_out", [P, 1], F32)
+        nc.vector.memset(warm_in[:], 0.0)
+        nc.scalar.activation(warm_out[:], warm_in[:], ACT.Sigmoid)
+
         def load_scale_rows(pool_bytes, scales):
             rows = scales[0].rearrange("(a f) c -> f a c", f=SCALE_ROWS)
             for f in range(SCALE_ROWS):

from contextlib import ExitStack

import concourse.mybir as mybir
from concourse.masks import make_identity

D, K, R, T, I, Q = 512, 512, 512, 2048, 512, 128
FLOPS = 2 * (D * Q * I + K * R * I + I * Q * R)

F32 = mybir.dt.float32
BF16 = mybir.dt.bfloat16
I32 = mybir.dt.int32
U32 = mybir.dt.uint32
U16 = mybir.dt.uint16
U8 = mybir.dt.uint8
FP8X4 = mybir.dt.float8_e4m3fn_x4
FP4X4 = mybir.dt.float4_e2m1fn_x4
ALU = mybir.AluOpType
ACT = mybir.ActivationFunctionType

P = 128
PACK = 4
QUADRANT = 32
SCALE_ROWS = 4
LIST_ROWS = 16
CHUNKS = R // P
LAST = CHUNKS - 1
TINY = 2.0 ** -60
ZH_BANKS = 3
TURN_BANKS = 2


def halves(n):
    return [slice(0, n // 2), slice(n // 2, n)]


def tile_attend_lrgained_capped_kernel(tc, query, keys_words, keys_scales, th, reserve, tab_words, tab_scales,
                                        w1, gain, slot_factor, value_scale, offs, out):
    nc = tc.nc
    with ExitStack() as ctx:
        keep = ctx.enter_context(tc.tile_pool(name="keep", bufs=1))
        psum = ctx.enter_context(tc.psum_pool(name="psum", bufs=1))

        def sbuf(name, shape, dtype, tag=None):
            return keep.tile(shape, dtype, name=name, tag=tag or name, align_bytes=64)

        def bank(name, shape, tag):
            return psum.tile(shape, F32, name=name, tag=tag, bufs={"zh": ZH_BANKS, "turned": TURN_BANKS}.get(tag, 1))

        def quantise(codes, scale_bytes, grouped):
            nc.vector.quantize_mx(codes.bitcast(FP8X4), scale_bytes, grouped.rearrange("p c t -> p (c t)"))

        offsets = keep.tile([P, I // LIST_ROWS], U16, name="offsets")
        nc.sync.dma_start(offsets[:], offs)

        key_pool_bytes = sbuf("key_pool_bytes", [P, T], U8)
        tab_pool_bytes = sbuf("tab_pool_bytes", [P, T], U8)
        nc.vector.memset(key_pool_bytes[:].bitcast(I32), 0)
        nc.vector.memset(tab_pool_bytes[:].bitcast(I32), 0)

        warm_in = sbuf("warm_in", [P, 1], F32)
        warm_out = sbuf("warm_out", [P, 1], F32)
        nc.vector.memset(warm_in[:], 0.0)
        nc.scalar.activation(warm_out[:], warm_in[:], ACT.Sigmoid)

        def load_scale_rows(pool_bytes, scales):
            rows = scales[0].rearrange("(a f) c -> f a c", f=SCALE_ROWS)
            for f in range(SCALE_ROWS):
                nc.sync.dma_start(pool_bytes[f:P:QUADRANT, :].bitcast(I32), rows[f].bitcast(I32))

        load_scale_rows(key_pool_bytes, keys_scales)
        key_pool_words = sbuf("key_pool_words", [P, T], U16)
        tab_pool_words = sbuf("tab_pool_words", [P, T], U16)
        query_rows = sbuf("query_rows", [P, PACK, Q], F32)
        nc.sync.dma_start(query_rows[:], query.rearrange("(p t) q -> p t q", t=PACK))
        nc.sync.dma_start(key_pool_words[:].bitcast(I32), keys_words[0].bitcast(I32))
        nc.sync.dma_start(tab_pool_words[:].bitcast(I32), tab_words[0].bitcast(I32))
        w1_rows = sbuf("w1_rows", [P, PACK, R], F32)
        load_scale_rows(tab_pool_bytes, tab_scales)
        nc.sync.dma_start(w1_rows[:], w1.rearrange("(p t) r -> p t r", t=PACK))

        th_col = sbuf("th_col", [P, 1], F32)
        reserve_col = sbuf("reserve_col", [P, 1], F32)
        os_cols = sbuf("os_cols", [P, PACK], F32)
        vs_cols = sbuf("vs_cols", [P, PACK], F32)
        gain_cols = sbuf("gain_cols", [P, CHUNKS], F32)
        with nc.allow_non_contiguous_dma(reason="one value a partition"):
            nc.gpsimd.dma_start(th_col[:], th)
        identity = sbuf("identity", [P, P], F32)
        make_identity(nc, identity[:])
        nc.gpsimd.dma_start(os_cols[:], slot_factor.rearrange("o (s t) -> s (o t)", t=PACK))
        nc.gpsimd.dma_start(vs_cols[:], value_scale.rearrange("o (s t) -> s (o t)", t=PACK))
        with nc.allow_non_contiguous_dma(reason="one value a partition (and chunk)"):
            nc.gpsimd.dma_start(reserve_col[:], reserve)
            nc.sync.dma_start(gain_cols[:], gain.rearrange("(c p) o -> p (c o)", p=P))

        key_bytes = sbuf("key_bytes", [P, I], U8)
        key_words = sbuf("key_words", [P, I], U16)
        nc.vector.tensor_copy(key_bytes[:], key_pool_bytes[:].indirect(offsets[:]))

        neg_query = sbuf("neg_query", [P, Q, PACK], BF16)
        nc.vector.tensor_scalar(neg_query[:], query_rows[:].rearrange("p t q -> p q t"), -1.0, None, ALU.mult)
        query_codes = sbuf("query_codes", [P, Q], U32)
        query_bytes = sbuf("query_bytes", [P, Q], U8)
        quantise(query_codes[:], query_bytes[:], neg_query[:])

        neg_a = [bank("neg_a0", [P, I // 2], "scores"), bank("neg_a1", [P, I // 2], "turned")]
        sigmoid = sbuf("sigmoid", [P, I], F32)
        for half_a, slots, columns in zip(neg_a, halves(I), halves(I // LIST_ROWS)):
            nc.vector.tensor_copy(key_words[:, slots], key_pool_words[:].indirect(offsets[:, columns]))
            nc.tensor.matmul_mx(half_a[:], lhsT=query_codes[:].bitcast(FP8X4), lhsT_scale=query_bytes[:],
                                rhs=key_words[:, slots].bitcast(FP4X4), rhs_scale=key_bytes[:, slots],
                                start=True, stop=True)
            nc.scalar.activation(sigmoid[:, slots], half_a[:], ACT.Sigmoid, bias=th_col[:])

        os_spread = bank("os_spread", [P, PACK, P], "os")
        vs_spread = bank("vs_spread", [P, PACK, P], "vs")
        for t in range(PACK):
            nc.tensor.transpose(os_spread[:, t, :], os_cols[:, t:t + 1].to_broadcast([P, P]), identity[:])
        for t in range(PACK):
            u, e = divmod(t, 2)
            nc.tensor.transpose(vs_spread[:, 2 * e + u, :], vs_cols[:, t:t + 1].to_broadcast([P, P]), identity[:])

        ln_sigmoid = sbuf("ln_sigmoid", [P, I], F32)
        nc.scalar.activation(ln_sigmoid[:], sigmoid[:], ACT.Ln, bias=TINY)

        tab_bytes = sbuf("tab_bytes", [P, I], U8)
        tab_listed_words = sbuf("tab_listed_words", [P, I], U16)
        nc.vector.tensor_copy(tab_listed_words[:], tab_pool_words[:].indirect(offsets[:]))
        nc.vector.tensor_copy(tab_bytes[:], tab_pool_bytes[:].indirect(offsets[:]))

        w1_codes = sbuf("w1_codes", [P, R], U32)
        w1_bytes = sbuf("w1_bytes", [P, R], U8)
        w1_grouped = [sbuf("w1_grouped%d" % h, [P, R // 2, PACK], BF16) for h in range(2)]
        for grouped, cols in zip(w1_grouped, halves(R)):
            nc.vector.tensor_copy(grouped[:].rearrange("p (c n) t -> p c t n", n=4),
                                  w1_rows[:, :, cols].rearrange("p t (c n) -> p c t n", n=4))
        first, second = halves(R)
        quantise(w1_codes[:, first], w1_bytes[:, first], w1_grouped[0][:])

        neg_p = sbuf("neg_p", [P, I], F32, tag="w1_rows")
        neg_sums = [sbuf("neg_sum%d" % h, [P, 1], F32) for h in range(2)]
        for half_a, slots, neg_sum in zip(neg_a, halves(I), neg_sums):
            nc.vector.scalar_tensor_tensor(neg_p[:, slots], half_a[:], th_col[:], ln_sigmoid[:, slots],
                                           ALU.add, ALU.min, accum_out=neg_sum[:])
        quantise(w1_codes[:, second], w1_bytes[:, second], w1_grouped[1][:])
        neg_z = sbuf("neg_z", [P, 1], F32)
        nc.vector.tensor_scalar(neg_z[:], neg_sums[0][:], neg_sums[1][:], reserve_col[:], ALU.add, ALU.subtract)
        neg_inv_z = sbuf("neg_inv_z", [P, 1], F32)
        nc.vector.reciprocal(neg_inv_z[:], neg_z[:])
        wo1 = sbuf("wo1", [P, I], BF16)
        nc.vector.scalar_tensor_tensor(wo1[:].rearrange("p (s t) -> p s t", t=PACK),
                                       neg_p[:].rearrange("p (s t) -> p s t", t=PACK), neg_inv_z[:],
                                       os_spread[:].rearrange("p t s -> p s t"), ALU.mult, ALU.mult)

        def turn(pairs, turned, grouped):
            for u in range(2):
                nc.tensor.transpose(turned[:, u, :], pairs[u], identity[:])
            nc.scalar.copy(grouped[:].bitcast(F32), turned[:].rearrange("s u x -> s x u"))

        ht = []
        for c in range(CHUNKS):
            cols = slice(c * P, (c + 1) * P)
            zh = bank("zh", [P, I], "zh")
            nc.tensor.matmul_mx(zh[:], lhsT=w1_codes[:, cols].bitcast(FP8X4), lhsT_scale=w1_bytes[:, cols],
                                rhs=tab_listed_words[:].bitcast(FP4X4), rhs_scale=tab_bytes[:], start=True, stop=True)
            ht.append(sbuf("ht%d" % c, [P, I], F32))
            nc.scalar.activation(ht[c][:].rearrange("p (u s e) -> p u s e", u=2, e=2),
                                 zh[:].rearrange("p (s u e) -> p u s e", u=2, e=2), ACT.Tanh)

        wt1_turned = bank("wt1_turned", [P, 2, Q], "zh")
        wt1_grouped = sbuf("wt1_grouped", [P, Q, PACK], BF16)
        turn([wo1[:].bitcast(F32)[:, u::2] for u in range(2)], wt1_turned, wt1_grouped)
        wt1_codes = sbuf("wt1_codes", [P, Q], U32)
        wt1_bytes = sbuf("wt1_bytes", [P, Q], U8)
        quantise(wt1_codes[:], wt1_bytes[:], wt1_grouped[:])

        ht1_grouped = []
        for c in range(CHUNKS):
            hw = sbuf("hw%d" % c, [P, I], BF16)
            for part in (halves(2 * P) if c == LAST else [slice(0, 2 * P)]):
                nc.vector.scalar_tensor_tensor(hw[:].rearrange("p (x e) -> p x e", e=2)[:, part, :],
                                               ht[c][:].rearrange("p (x e) -> p x e", e=2)[:, part, :],
                                               gain_cols[:, c:c + 1],
                                               vs_spread[:].rearrange("p (e u) s -> p (u s) e", e=2)[:, part, :],
                                               ALU.mult, ALU.mult)
            ht1_turned = bank("ht1_turned", [P, 2, P], "turned")
            ht1_grouped.append(sbuf("ht1_grouped%d" % c, [P, P, PACK], BF16))
            turn([hw[:].bitcast(F32)[:, part] for part in halves(2 * P)], ht1_turned, ht1_grouped[c])

        result = sbuf("result", [P, R], F32)
        for c in range(CHUNKS):
            cols = slice(c * P, (c + 1) * P)
            ht1_codes = sbuf("ht1_codes%d" % c, [P, P], U32)
            ht1_bytes = sbuf("ht1_bytes%d" % c, [P, P], U8)
            quantise(ht1_codes[:], ht1_bytes[:], ht1_grouped[c][:])
            sums = bank("sums", [P, P], ("os", "scores")[c % 2])
            nc.tensor.matmul_mx(sums[:], lhsT=wt1_codes[:].bitcast(FP8X4), lhsT_scale=wt1_bytes[:],
                                rhs=ht1_codes[:].bitcast(FP8X4), rhs_scale=ht1_bytes[:], start=True, stop=True)
            nc.scalar.copy(result[:, cols], sums[:])
            if c == LAST - 1:
                nc.sync.dma_start(out[:, 0:LAST * P], result[:, 0:LAST * P])
        nc.scalar.dma_start(out[:, LAST * P:R], result[:, LAST * P:R])
